import numpy as np
import ml_dtypes


def mxq(x, axis, fmt="e4m3"):
    dtype, down = {"e4m3": (ml_dtypes.float8_e4m3fn, 7), "e5m2": (ml_dtypes.float8_e5m2, 14)}[fmt]
    v = np.moveaxis(np.asarray(x, np.float32).astype(ml_dtypes.bfloat16).astype(np.float64), axis, -1)
    blocks = v.reshape(v.shape[:-1] + (-1, 32))
    amax = np.abs(blocks).max(-1, keepdims=True)
    byte = np.maximum(np.where(amax > 0, np.frexp(amax)[1] - 1 + 127, 0) - down, 1)
    scale = np.exp2(byte - 127.0)
    codes = (blocks / scale).astype(np.float32).astype(dtype).astype(np.float64)
    return np.moveaxis((codes * scale).reshape(v.shape), -1, axis)


WIDE = False


def mx_kscale(k):
    if not WIDE:
        return np.ones(k)
    levels = np.array([10, -10, 5, -5, 0])
    if k % 512:
        return np.exp2(np.random.permutation(np.resize(levels, k // 32))).repeat(32)
    a = np.empty((k // 512, 16))
    for p in range(k // 512):
        a[p, :8] = np.random.permutation(np.resize(levels, 8))
        for g in range(8):
            far = levels[np.abs(levels - a[p, g]) >= 10]
            a[p, g + 8] = far[np.random.randint(len(far))]
    return np.exp2(a.ravel()).repeat(32)


def f64(x):
    return np.asarray(x).astype(np.float64)


def striped(idx):
    return np.tile(idx.reshape(-1, 16).T, (8, 1)).astype(np.uint16)


def unstriped(offs):
    return offs[:16].T.reshape(-1).astype(np.int64)


E2M1 = np.array([0.0, 0.5, 1.0, 1.5, 2.0, 3.0, 4.0, 6.0, -0.0, -0.5, -1.0, -1.5, -2.0, -3.0, -4.0, -6.0])


def pack_weight(w, fmt):
    k, n = w.shape
    w = f64(np.asarray(w, np.float32).astype(ml_dtypes.bfloat16)).reshape(k // 32, 32, n)
    amax = np.abs(w).max(1)
    if fmt == "e4m3":
        byte = np.frexp(amax)[1] - 1 + 127 - 7
    else:
        mant, ex = np.frexp(amax / 6.0)
        byte = np.where(mant > 0.5, ex, ex - 1) + 127
    byte = np.clip(np.where(amax > 0, byte, 1), 1, 254)
    scaled = (w * np.exp2(127.0 - byte)[:, None, :]).reshape(k, n).astype(np.float32)
    by_word = np.ascontiguousarray(scaled.reshape(k // 512, 128, 4, n).transpose(0, 1, 3, 2))
    if fmt == "e4m3":
        words = by_word.astype(ml_dtypes.float8_e4m3fn).view(np.uint8)
    else:
        c = by_word.astype(ml_dtypes.float4_e2m1fn).view(np.uint8) & 0xF
        words = (c[..., 0::2] | (c[..., 1::2] << 4)).reshape(k // 512, 128, 2 * n)
    return np.ascontiguousarray(words), np.ascontiguousarray(byte.astype(np.uint8).reshape(k // 512, 16, n))


def unpack_weight(words, scales, fmt):
    g, _, n = scales.shape
    words = np.ascontiguousarray(words).reshape(g, 128, n, -1)
    if fmt == "e4m3":
        vals = words.view(ml_dtypes.float8_e4m3fn).astype(np.float64)
    else:
        nib = np.empty((g, 128, n, 4), np.uint8)
        nib[..., 0::2] = words & 0xF
        nib[..., 1::2] = words >> 4
        vals = E2M1[nib]
    vals = vals * np.repeat(np.exp2(scales.astype(np.float64) - 127.0), 8, axis=1)[..., None]
    return vals.transpose(0, 1, 3, 2).reshape(g * 512, n)


def pack_table(v):
    words, scales = pack_weight(v, "e4m3")
    return np.concatenate([words.reshape(words.shape[0], -1), scales.reshape(scales.shape[0], -1)], axis=1)


def unpack_table(tab):
    g, t = tab.shape[0], tab.shape[1] // 528
    return unpack_weight(tab[:, :512 * t].reshape(g, 128, t, 4), tab[:, 512 * t:].reshape(g, 16, t), "e4m3")


O, K, M, T, S = 512, 1024, 128, 4096, 1024


def setup_inputs():
    n = np.random.standard_normal
    s = mx_kscale(K)[:, None]
    w = n((K, M)) / np.sqrt(K) / s
    p_w4 = pack_weight(w[O:], "e2m1")
    return {
        "tab": pack_table(n((K, T)) * s),
        "w8": (w[:O]).astype(np.float32),
        "w4_words": p_w4[0],
        "w4_scales": p_w4[1],
        "gate": (n((128, 1024))).astype(np.float32),
        "offs": striped(np.random.permutation(T)[:S]),
    }


def reference(tab, w8, w4_words, w4_scales, gate, offs):
    tab_ = unpack_table(tab)[:, unstriped(offs)]
    w8_ = mxq(f64(w8), 0, "e4m3")
    w4_ = unpack_weight(w4_words, w4_scales, "e2m1")
    y = w8_.T @ tab_[:O] + w4_.T @ tab_[O:]
    return f64(gate) * y

@@ -1,0 +1,105 @@
+from contextlib import ExitStack
+
+import concourse.mybir as mybir
+
+O, K, M, T, S = 512, 1024, 128, 4096, 1024
+FLOPS = 2 * K * M * S
+
+P = 128
+PACK = 4
+HALF = 512
+
+F32 = mybir.dt.float32
+BF16 = mybir.dt.bfloat16
+I32 = mybir.dt.int32
+U32 = mybir.dt.uint32
+U16 = mybir.dt.uint16
+U8 = mybir.dt.uint8
+E4M3X4 = mybir.dt.float8_e4m3fn_x4
+E2M1X4 = mybir.dt.float4_e2m1fn_x4
+MULT = mybir.AluOpType.mult
+
+
+def tile_list_tabo_mul_kernel(tc, tab, w8, w4_words, w4_scales, gate, offs, out):
+    nc = tc.nc
+    with ExitStack() as ctx:
+        keep = ctx.enter_context(tc.tile_pool(name="keep", bufs=1))
+        psum = ctx.enter_context(tc.psum_pool(name="psum", bufs=1))
+
+        offsets = keep.tile([P, S // 16], U16, name="offsets")
+        planes = keep.tile([P, T], U8, name="planes", align_bytes=64)
+        words = [keep.tile([P, T], I32, name=f"words{a}", align_bytes=64) for a in range(2)]
+        picked = [keep.tile([P, S], U32, name=f"picked{a}", align_bytes=64) for a in range(2)]
+        picked_planes = keep.tile([P, S], U8, name="picked_planes", align_bytes=64)
+        w8_raw = keep.tile([P, PACK, M], F32, name="w8_raw", tag="staged")
+        w8_grouped = keep.tile([P, M, PACK], BF16, name="w8_grouped", align_bytes=64)
+        w8_codes = keep.tile([P, M], U32, name="w8_codes", align_bytes=64)
+        w8_plane = keep.tile([P, M], U8, name="w8_plane", align_bytes=64)
+        w4_codes = keep.tile([P, 2 * M], U8, name="w4_codes", align_bytes=64)
+        w4_plane = keep.tile([P, M], U8, name="w4_plane", align_bytes=64)
+
+        nc.sync.dma_start(offsets[:], offs)
+        nc.vector.memset(planes[:].bitcast(I32), 0)
+        nc.vector.memset(w4_plane[:].bitcast(I32), 0)
+
+        def load_words(a):
+            nc.sync.dma_start(words[a][:], tab[a, 0 : 512 * T].rearrange("(p x) -> p x", p=P).bitcast(I32))
+
+        rows = [tab[a, 512 * T : 528 * T].rearrange("(q t) -> q t", q=16) for a in range(2)]
+
+        def load_plane_rows(queue, a, q):
+            first = 32 * q + (4 if a == 0 else 0)
+            queue.dma_start(planes[first : first + 4, :].bitcast(I32), rows[a][4 * q : 4 * q + 4, :].bitcast(I32))
+
+        nc.gpsimd.dma_start(w8_raw[:], w8.rearrange("(p j) n -> p j n", j=PACK))
+        load_words(0)
+        load_words(1)
+        for a, q in [(0, 0), (0, 1), (0, 2), (0, 3), (1, 0)]:
+            load_plane_rows(nc.scalar, a, q)
+        for a, q in [(1, 1), (1, 2), (1, 3)]:
+            load_plane_rows(nc.gpsimd, a, q)
+        nc.gpsimd.dma_start(w4_codes[:].bitcast(I32), w4_words[0].bitcast(I32))
+        for q in range(4):
+            nc.gpsimd.dma_start(
+                w4_plane[32 * q : 32 * q + 4, :].bitcast(I32), w4_scales[0, 4 * q : 4 * q + 4, :].bitcast(I32)
+            )
+
+        nc.scalar.copy(out=w8_grouped[:], in_=w8_raw[:].rearrange("p j n -> p n j"))
+        gates = keep.tile([P, S], F32, name="gates", tag="staged")
+        nc.sync.dma_start(gates[:], gate)
+
+        nc.vector.tensor_copy(picked_planes[:], planes[:].indirect(offsets[:]))
+        nc.vector.tensor_copy(picked[0][:], words[0][:].bitcast(U32).indirect(offsets[:]))
+        nc.vector.quantize_mx(
+            out=w8_codes[:].bitcast(E4M3X4), scales=w8_plane[:], in_=w8_grouped[:].rearrange("p n j -> p (n j)")
+        )
+        halves = [slice(h * HALF, (h + 1) * HALF) for h in range(2)]
+        banks = [psum.tile([M, HALF], F32, name=f"bank{h}") for h in range(2)]
+        for h in range(2):
+            nc.tensor.matmul_mx(
+                out=banks[h][:],
+                lhsT=w8_codes[:].bitcast(E4M3X4),
+                lhsT_scale=w8_plane[:],
+                rhs=picked[0][:, halves[h]].bitcast(E4M3X4),
+                rhs_scale=picked_planes[4:P, halves[h]],
+                start=True,
+                stop=False,
+            )
+        for h in range(2):
+            nc.vector.tensor_copy(
+                picked[1][:, halves[h]],
+                words[1][:].bitcast(U32).indirect(offsets[:, h * HALF // 16 : (h + 1) * HALF // 16]),
+            )
+            nc.tensor.matmul_mx(
+                out=banks[h][:],
+                lhsT=w4_codes[:].bitcast(E2M1X4),
+                lhsT_scale=w4_plane[:],
+                rhs=picked[1][:, halves[h]].bitcast(E4M3X4),
+                rhs_scale=picked_planes[:, halves[h]],
+                start=False,
+                stop=True,
+            )
+        for h in range(2):
+            result = keep.tile([M, HALF], F32, name=f"result{h}")
+            nc.vector.tensor_tensor(result[:], banks[h][:], gates[:, halves[h]], MULT)
+            nc.sync.dma_start(out[:, halves[h]], result[:])

@@ -8,6 +8,7 @@ FLOPS = 2 * K * M * S
 P = 128
 PACK = 4
 HALF = 512
+HEAD = 1024
 
 F32 = mybir.dt.float32
 BF16 = mybir.dt.bfloat16
@@ -27,40 +28,38 @@ def tile_list_tabo_mul_kernel(tc, tab, w8, w4_words, w4_scales, gate, offs, out)
         psum = ctx.enter_context(tc.psum_pool(name="psum", bufs=1))
 
         offsets = keep.tile([P, S // 16], U16, name="offsets")
-        planes = keep.tile([P, T], U8, name="planes", align_bytes=64)
+        planes = keep.tile([P, T], U8, name="planes", tag="planes", align_bytes=64)
         words = [keep.tile([P, T], I32, name=f"words{a}", align_bytes=64) for a in range(2)]
-        picked = [keep.tile([P, S], U32, name=f"picked{a}", align_bytes=64) for a in range(2)]
+        picked = [keep.tile([P, S], U32, name="picked0", align_bytes=64)]
         picked_planes = keep.tile([P, S], U8, name="picked_planes", align_bytes=64)
         w8_raw = keep.tile([P, PACK, M], F32, name="w8_raw", tag="staged")
         w8_grouped = keep.tile([P, M, PACK], BF16, name="w8_grouped", align_bytes=64)
         w8_codes = keep.tile([P, M], U32, name="w8_codes", align_bytes=64)
         w8_plane = keep.tile([P, M], U8, name="w8_plane", align_bytes=64)
-        w4_codes = keep.tile([P, 2 * M], U8, name="w4_codes", align_bytes=64)
-        w4_plane = keep.tile([P, M], U8, name="w4_plane", align_bytes=64)
+        w4_bytes = keep.tile([P, 3 * M], U8, name="w4_bytes", align_bytes=64)
+        w4_codes, w4_plane = w4_bytes[:, 0 : 2 * M], w4_bytes[:, 2 * M : 3 * M]
 
-        nc.sync.dma_start(offsets[:], offs)
+        word_rows = [tab[a, 0 : 512 * T].rearrange("(p x) -> p x", p=P) for a in range(2)]
+        scale_rows = [tab[a, 512 * T : 528 * T].rearrange("(q t) -> q t", q=16) for a in range(2)]
+
         nc.vector.memset(planes[:].bitcast(I32), 0)
-        nc.vector.memset(w4_plane[:].bitcast(I32), 0)
+        nc.vector.memset(words[1][:, 0:HEAD], 0)
+        nc.vector.memset(w4_bytes[:].bitcast(I32), 0)
 
-        def load_words(a):
-            nc.sync.dma_start(words[a][:], tab[a, 0 : 512 * T].rearrange("(p x) -> p x", p=P).bitcast(I32))
-
-        rows = [tab[a, 512 * T : 528 * T].rearrange("(q t) -> q t", q=16) for a in range(2)]
-
-        def load_plane_rows(queue, a, q):
-            first = 32 * q + (4 if a == 0 else 0)
-            queue.dma_start(planes[first : first + 4, :].bitcast(I32), rows[a][4 * q : 4 * q + 4, :].bitcast(I32))
-
+        nc.sync.dma_start(words[0][:], word_rows[0].bitcast(I32))
+        nc.sync.dma_start(offsets[:], offs)
+        for a in range(2):
+            for q in range(4):
+                first = 32 * q + (4 if a == 0 else 0)
+                queue = nc.scalar if 4 * a + q < 5 else nc.gpsimd
+                queue.dma_start(
+                    planes[first : first + 4, :].bitcast(I32), scale_rows[a][4 * q : 4 * q + 4, :].bitcast(I32)
+                )
+        nc.sync.dma_start(words[1][:], word_rows[1].bitcast(I32))
         nc.gpsimd.dma_start(w8_raw[:], w8.rearrange("(p j) n -> p j n", j=PACK))
-        load_words(0)
-        load_words(1)
-        for a, q in [(0, 0), (0, 1), (0, 2), (0, 3), (1, 0)]:
-            load_plane_rows(nc.scalar, a, q)
-        for a, q in [(1, 1), (1, 2), (1, 3)]:
-            load_plane_rows(nc.gpsimd, a, q)
-        nc.gpsimd.dma_start(w4_codes[:].bitcast(I32), w4_words[0].bitcast(I32))
+        nc.scalar.dma_start(w4_codes.bitcast(I32), w4_words[0].bitcast(I32))
         for q in range(4):
-            nc.gpsimd.dma_start(
+            nc.scalar.dma_start(
                 w4_plane[32 * q : 32 * q + 4, :].bitcast(I32), w4_scales[0, 4 * q : 4 * q + 4, :].bitcast(I32)
             )
 
@@ -69,6 +68,7 @@ def tile_list_tabo_mul_kernel(tc, tab, w8, w4_words, w4_scales, gate, offs, out)
         nc.sync.dma_start(gates[:], gate)
 
         nc.vector.tensor_copy(picked_planes[:], planes[:].indirect(offsets[:]))
+        picked.append(keep.tile([P, S], U32, name="picked1", tag="planes", align_bytes=64))
         nc.vector.tensor_copy(picked[0][:], words[0][:].bitcast(U32).indirect(offsets[:]))
         nc.vector.quantize_mx(
             out=w8_codes[:].bitcast(E4M3X4), scales=w8_plane[:], in_=w8_grouped[:].rearrange("p n j -> p (n j)")
@@ -92,8 +92,8 @@ def tile_list_tabo_mul_kernel(tc, tab, w8, w4_words, w4_scales, gate, offs, out)
             )
             nc.tensor.matmul_mx(
                 out=banks[h][:],
-                lhsT=w4_codes[:].bitcast(E2M1X4),
-                lhsT_scale=w4_plane[:],
+                lhsT=w4_codes.bitcast(E2M1X4),
+                lhsT_scale=w4_plane,
                 rhs=picked[1][:, halves[h]].bitcast(E4M3X4),
                 rhs_scale=picked_planes[:, halves[h]],
                 start=False,

@@ -8,7 +8,7 @@ FLOPS = 2 * K * M * S
 P = 128
 PACK = 4
 HALF = 512
-HEAD = 1024
+QUARTER = T // 4
 
 F32 = mybir.dt.float32
 BF16 = mybir.dt.bfloat16
@@ -29,7 +29,7 @@ def tile_list_tabo_mul_kernel(tc, tab, w8, w4_words, w4_scales, gate, offs, out)
 
         offsets = keep.tile([P, S // 16], U16, name="offsets")
         planes = keep.tile([P, T], U8, name="planes", tag="planes", align_bytes=64)
-        words = [keep.tile([P, T], I32, name=f"words{a}", align_bytes=64) for a in range(2)]
+        words = keep.tile([P, 2 * T], I32, name="words", align_bytes=64)
         picked = [keep.tile([P, S], U32, name="picked0", align_bytes=64)]
         picked_planes = keep.tile([P, S], U8, name="picked_planes", align_bytes=64)
         w8_raw = keep.tile([P, PACK, M], F32, name="w8_raw", tag="staged")
@@ -43,23 +43,35 @@ def tile_list_tabo_mul_kernel(tc, tab, w8, w4_words, w4_scales, gate, offs, out)
         scale_rows = [tab[a, 512 * T : 528 * T].rearrange("(q t) -> q t", q=16) for a in range(2)]
 
         nc.vector.memset(planes[:].bitcast(I32), 0)
-        nc.vector.memset(words[1][:, 0:HEAD], 0)
+        nc.vector.memset(words[:, 2 * QUARTER : 6 * QUARTER : 2 * QUARTER], 0)
         nc.vector.memset(w4_bytes[:].bitcast(I32), 0)
 
-        nc.sync.dma_start(words[0][:], word_rows[0].bitcast(I32))
-        nc.sync.dma_start(offsets[:], offs)
-        for a in range(2):
-            for q in range(4):
-                first = 32 * q + (4 if a == 0 else 0)
-                queue = nc.scalar if 4 * a + q < 5 else nc.gpsimd
-                queue.dma_start(
-                    planes[first : first + 4, :].bitcast(I32), scale_rows[a][4 * q : 4 * q + 4, :].bitcast(I32)
+        def load_words(first, last):
+            a, start = divmod(first, 4)
+            stop = start + last - first
+            nc.sync.dma_start(
+                words[:, first * QUARTER : last * QUARTER],
+                word_rows[a][:, 4 * start * QUARTER : 4 * stop * QUARTER].bitcast(I32),
+            )
+
+        def load_scale_rows(first, last):
+            for a, q in [(i // 4, i % 4) for i in range(first, last)]:
+                row = 32 * q + (4 if a == 0 else 0)
+                nc.sync.dma_start(
+                    planes[row : row + 4, :].bitcast(I32), scale_rows[a][4 * q : 4 * q + 4, :].bitcast(I32)
                 )
-        nc.sync.dma_start(words[1][:], word_rows[1].bitcast(I32))
+
         nc.gpsimd.dma_start(w8_raw[:], w8.rearrange("(p j) n -> p j n", j=PACK))
-        nc.scalar.dma_start(w4_codes.bitcast(I32), w4_words[0].bitcast(I32))
+        nc.gpsimd.dma_start(w4_codes.bitcast(I32), w4_words[0].bitcast(I32))
+        nc.sync.dma_start(offsets[:], offs)
+        load_words(0, 1)
+        load_words(1, 2)
+        load_scale_rows(0, 5)
+        load_words(2, 4)
+        load_scale_rows(5, 8)
+        load_words(4, 8)
         for q in range(4):
-            nc.scalar.dma_start(
+            nc.sync.dma_start(
                 w4_plane[32 * q : 32 * q + 4, :].bitcast(I32), w4_scales[0, 4 * q : 4 * q + 4, :].bitcast(I32)
             )
 
@@ -69,7 +81,7 @@ def tile_list_tabo_mul_kernel(tc, tab, w8, w4_words, w4_scales, gate, offs, out)
 
         nc.vector.tensor_copy(picked_planes[:], planes[:].indirect(offsets[:]))
         picked.append(keep.tile([P, S], U32, name="picked1", tag="planes", align_bytes=64))
-        nc.vector.tensor_copy(picked[0][:], words[0][:].bitcast(U32).indirect(offsets[:]))
+        nc.vector.tensor_copy(picked[0][:], words[:, 0:T].bitcast(U32).indirect(offsets[:]))
         nc.vector.quantize_mx(
             out=w8_codes[:].bitcast(E4M3X4), scales=w8_plane[:], in_=w8_grouped[:].rearrange("p n j -> p (n j)")
         )
@@ -88,7 +100,7 @@ def tile_list_tabo_mul_kernel(tc, tab, w8, w4_words, w4_scales, gate, offs, out)
         for h in range(2):
             nc.vector.tensor_copy(
                 picked[1][:, halves[h]],
-                words[1][:].bitcast(U32).indirect(offsets[:, h * HALF // 16 : (h + 1) * HALF // 16]),
+                words[:, T : 2 * T].bitcast(U32).indirect(offsets[:, h * HALF // 16 : (h + 1) * HALF // 16]),
             )
             nc.tensor.matmul_mx(
                 out=banks[h][:],

@@ -43,7 +43,7 @@ def tile_list_tabo_mul_kernel(tc, tab, w8, w4_words, w4_scales, gate, offs, out)
         scale_rows = [tab[a, 512 * T : 528 * T].rearrange("(q t) -> q t", q=16) for a in range(2)]
 
         nc.vector.memset(planes[:].bitcast(I32), 0)
-        nc.vector.memset(words[:, 2 * QUARTER : 6 * QUARTER : 2 * QUARTER], 0)
+        nc.vector.memset(words[:, QUARTER : 5 * QUARTER : QUARTER], 0)
         nc.vector.memset(w4_bytes[:].bitcast(I32), 0)
 
         def load_words(first, last):
@@ -55,20 +55,18 @@ def tile_list_tabo_mul_kernel(tc, tab, w8, w4_words, w4_scales, gate, offs, out)
             )
 
         def load_scale_rows(first, last):
-            for a, q in [(i // 4, i % 4) for i in range(first, last)]:
-                row = 32 * q + (4 if a == 0 else 0)
-                nc.sync.dma_start(
-                    planes[row : row + 4, :].bitcast(I32), scale_rows[a][4 * q : 4 * q + 4, :].bitcast(I32)
-                )
+            for r, a in [divmod(i, 2) for i in range(first, last)]:
+                row = r + (4 if a == 0 else 0)
+                nc.sync.dma_start(planes[row:P:32, :].bitcast(I32), scale_rows[a][r:16:4, :].bitcast(I32))
 
         nc.gpsimd.dma_start(w8_raw[:], w8.rearrange("(p j) n -> p j n", j=PACK))
         nc.gpsimd.dma_start(w4_codes.bitcast(I32), w4_words[0].bitcast(I32))
         nc.sync.dma_start(offsets[:], offs)
         load_words(0, 1)
-        load_words(1, 2)
         load_scale_rows(0, 5)
-        load_words(2, 4)
+        load_words(1, 3)
         load_scale_rows(5, 8)
+        load_words(3, 4)
         load_words(4, 8)
         for q in range(4):
             nc.sync.dma_start(

from contextlib import ExitStack

import concourse.mybir as mybir

O, K, M, T, S = 512, 1024, 128, 4096, 1024
FLOPS = 2 * K * M * S

P = 128
PACK = 4
HALF = 512
QUARTER = T // 4

F32 = mybir.dt.float32
BF16 = mybir.dt.bfloat16
I32 = mybir.dt.int32
U32 = mybir.dt.uint32
U16 = mybir.dt.uint16
U8 = mybir.dt.uint8
E4M3X4 = mybir.dt.float8_e4m3fn_x4
E2M1X4 = mybir.dt.float4_e2m1fn_x4
MULT = mybir.AluOpType.mult


def tile_list_tabo_mul_kernel(tc, tab, w8, w4_words, w4_scales, gate, offs, out):
    nc = tc.nc
    with ExitStack() as ctx:
        keep = ctx.enter_context(tc.tile_pool(name="keep", bufs=1))
        psum = ctx.enter_context(tc.psum_pool(name="psum", bufs=1))

        offsets = keep.tile([P, S // 16], U16, name="offsets")
        planes = keep.tile([P, T], U8, name="planes", tag="planes", align_bytes=64)
        words = keep.tile([P, 2 * T], I32, name="words", align_bytes=64)
        picked = [keep.tile([P, S], U32, name="picked0", align_bytes=64)]
        picked_planes = keep.tile([P, S], U8, name="picked_planes", align_bytes=64)
        w8_raw = keep.tile([P, PACK, M], F32, name="w8_raw", tag="staged")
        w8_grouped = keep.tile([P, M, PACK], BF16, name="w8_grouped", align_bytes=64)
        w8_codes = keep.tile([P, M], U32, name="w8_codes", align_bytes=64)
        w8_plane = keep.tile([P, M], U8, name="w8_plane", align_bytes=64)
        w4_bytes = keep.tile([P, 3 * M], U8, name="w4_bytes", align_bytes=64)
        w4_codes, w4_plane = w4_bytes[:, 0 : 2 * M], w4_bytes[:, 2 * M : 3 * M]

        word_rows = [tab[a, 0 : 512 * T].rearrange("(p x) -> p x", p=P) for a in range(2)]
        scale_rows = [tab[a, 512 * T : 528 * T].rearrange("(q t) -> q t", q=16) for a in range(2)]

        nc.vector.memset(planes[:].bitcast(I32), 0)
        nc.vector.memset(words[:, QUARTER : 5 * QUARTER : QUARTER], 0)
        nc.vector.memset(w4_bytes[:].bitcast(I32), 0)

        def load_words(first, last):
            a, start = divmod(first, 4)
            stop = start + last - first
            nc.sync.dma_start(
                words[:, first * QUARTER : last * QUARTER],
                word_rows[a][:, 4 * start * QUARTER : 4 * stop * QUARTER].bitcast(I32),
            )

        def load_scale_rows(first, last):
            for r, a in [divmod(i, 2) for i in range(first, last)]:
                row = r + (4 if a == 0 else 0)
                nc.sync.dma_start(planes[row:P:32, :].bitcast(I32), scale_rows[a][r:16:4, :].bitcast(I32))

        nc.gpsimd.dma_start(w8_raw[:], w8.rearrange("(p j) n -> p j n", j=PACK))
        nc.gpsimd.dma_start(w4_codes.bitcast(I32), w4_words[0].bitcast(I32))
        nc.sync.dma_start(offsets[:], offs)
        load_words(0, 1)
        load_scale_rows(0, 5)
        load_words(1, 3)
        load_scale_rows(5, 8)
        load_words(3, 4)
        load_words(4, 8)
        for q in range(4):
            nc.sync.dma_start(
                w4_plane[32 * q : 32 * q + 4, :].bitcast(I32), w4_scales[0, 4 * q : 4 * q + 4, :].bitcast(I32)
            )

        nc.scalar.copy(out=w8_grouped[:], in_=w8_raw[:].rearrange("p j n -> p n j"))
        gates = keep.tile([P, S], F32, name="gates", tag="staged")
        nc.sync.dma_start(gates[:], gate)

        nc.vector.tensor_copy(picked_planes[:], planes[:].indirect(offsets[:]))
        picked.append(keep.tile([P, S], U32, name="picked1", tag="planes", align_bytes=64))
        nc.vector.tensor_copy(picked[0][:], words[:, 0:T].bitcast(U32).indirect(offsets[:]))
        nc.vector.quantize_mx(
            out=w8_codes[:].bitcast(E4M3X4), scales=w8_plane[:], in_=w8_grouped[:].rearrange("p n j -> p (n j)")
        )
        halves = [slice(h * HALF, (h + 1) * HALF) for h in range(2)]
        banks = [psum.tile([M, HALF], F32, name=f"bank{h}") for h in range(2)]
        for h in range(2):
            nc.tensor.matmul_mx(
                out=banks[h][:],
                lhsT=w8_codes[:].bitcast(E4M3X4),
                lhsT_scale=w8_plane[:],
                rhs=picked[0][:, halves[h]].bitcast(E4M3X4),
                rhs_scale=picked_planes[4:P, halves[h]],
                start=True,
                stop=False,
            )
        for h in range(2):
            nc.vector.tensor_copy(
                picked[1][:, halves[h]],
                words[:, T : 2 * T].bitcast(U32).indirect(offsets[:, h * HALF // 16 : (h + 1) * HALF // 16]),
            )
            nc.tensor.matmul_mx(
                out=banks[h][:],
                lhsT=w4_codes.bitcast(E2M1X4),
                lhsT_scale=w4_plane,
                rhs=picked[1][:, halves[h]].bitcast(E4M3X4),
                rhs_scale=picked_planes[:, halves[h]],
                start=False,
                stop=True,
            )
        for h in range(2):
            result = keep.tile([M, HALF], F32, name=f"result{h}")
            nc.vector.tensor_tensor(result[:], banks[h][:], gates[:, halves[h]], MULT)
            nc.sync.dma_start(out[:, halves[h]], result[:])
